import numpy as np
import ml_dtypes


def mxq(x, axis, fmt="e4m3"):
    dtype, down = {"e4m3": (ml_dtypes.float8_e4m3fn, 7), "e5m2": (ml_dtypes.float8_e5m2, 14)}[fmt]
    v = np.moveaxis(np.asarray(x, np.float32).astype(ml_dtypes.bfloat16).astype(np.float64), axis, -1)
    blocks = v.reshape(v.shape[:-1] + (-1, 32))
    amax = np.abs(blocks).max(-1, keepdims=True)
    byte = np.maximum(np.where(amax > 0, np.frexp(amax)[1] - 1 + 127, 0) - down, 1)
    scale = np.exp2(byte - 127.0)
    codes = (blocks / scale).astype(np.float32).astype(dtype).astype(np.float64)
    return np.moveaxis((codes * scale).reshape(v.shape), -1, axis)


WIDE = False


def mx_kscale(k):
    if not WIDE:
        return np.ones(k)
    levels = np.array([10, -10, 5, -5, 0])
    if k % 512:
        return np.exp2(np.random.permutation(np.resize(levels, k // 32))).repeat(32)
    a = np.empty((k // 512, 16))
    for p in range(k // 512):
        a[p, :8] = np.random.permutation(np.resize(levels, 8))
        for g in range(8):
            far = levels[np.abs(levels - a[p, g]) >= 10]
            a[p, g + 8] = far[np.random.randint(len(far))]
    return np.exp2(a.ravel()).repeat(32)


def f64(x):
    return np.asarray(x).astype(np.float64)


def striped(idx):
    return np.tile(np.asarray(idx).reshape(-1, 16).T, (8, 1)).astype(np.uint16)


def unstriped(offs):
    return offs[:16].T.reshape(-1).astype(np.int64)


E2M1 = np.array([0.0, 0.5, 1.0, 1.5, 2.0, 3.0, 4.0, 6.0, -0.0, -0.5, -1.0, -1.5, -2.0, -3.0, -4.0, -6.0])


def pack_weight(w, fmt):
    k, n = w.shape
    w = f64(np.asarray(w, np.float32).astype(ml_dtypes.bfloat16)).reshape(k // 32, 32, n)
    amax = np.abs(w).max(1)
    if fmt == "e4m3":
        byte = np.frexp(amax)[1] - 1 + 127 - 7
    else:
        mant, ex = np.frexp(amax / 6.0)
        byte = np.where(mant > 0.5, ex, ex - 1) + 127
    byte = np.clip(np.where(amax > 0, byte, 1), 1, 254)
    scaled = (w * np.exp2(127.0 - byte)[:, None, :]).reshape(k, n).astype(np.float32)
    by_word = np.ascontiguousarray(scaled.reshape(k // 512, 128, 4, n).transpose(0, 1, 3, 2))
    if fmt == "e4m3":
        words = by_word.astype(ml_dtypes.float8_e4m3fn).view(np.uint8)
    else:
        c = by_word.astype(ml_dtypes.float4_e2m1fn).view(np.uint8) & 0xF
        words = (c[..., 0::2] | (c[..., 1::2] << 4)).reshape(k // 512, 128, 2 * n)
    return np.ascontiguousarray(words), np.ascontiguousarray(byte.astype(np.uint8).reshape(k // 512, 16, n))


def unpack_weight(words, scales, fmt):
    g, _, n = scales.shape
    words = np.ascontiguousarray(words).reshape(g, 128, n, -1)
    if fmt == "e4m3":
        vals = words.view(ml_dtypes.float8_e4m3fn).astype(np.float64)
    else:
        nib = np.empty((g, 128, n, 4), np.uint8)
        nib[..., 0::2] = words & 0xF
        nib[..., 1::2] = words >> 4
        vals = E2M1[nib]
    vals = vals * np.repeat(np.exp2(scales.astype(np.float64) - 127.0), 8, axis=1)[..., None]
    return vals.transpose(0, 1, 3, 2).reshape(g * 512, n)


def sigmoid(v):
    return 1.0 / (1.0 + np.exp(-v))


D, K, R, T, I, Q, G = 512, 512, 512, 2048, 512, 128, 32


def setup_inputs():
    n = np.random.standard_normal
    idx = np.random.permutation(T)[:I]
    fd = mx_kscale(D)
    fk = mx_kscale(K)
    fi = mx_kscale(I)
    keysp = pack_weight(n((D, T)) / fd[:, None], "e4m3")
    tabp = pack_weight(n((K, T)) / fk[:, None], "e4m3")
    return {
        "query": (n((D, Q)) * 0.6 / np.sqrt(D) * fd[:, None]).astype(np.float32),
        "query2": (n((D, Q)) * 1.0 / np.sqrt(D) * fd[:, None]).astype(np.float32),
        "keys_words": keysp[0],
        "keys_scales": keysp[1],
        "tab_words": tabp[0],
        "tab_scales": tabp[1],
        "w1": (n((K, R)) * 1 / np.sqrt(K) * fk[:, None]).astype(np.float32),
        "share": (np.random.uniform(0.4, 1.0, (R, 1))).astype(np.float32),
        "os": (np.random.uniform(4.0, 16.0, (1, I)) * fi).astype(np.float32),
        "vs": (np.random.uniform(0.5, 2.0, (1, I)) / fi).astype(np.float32),
        "offs": striped(idx),
    }


def reference(query, query2, keys_words, keys_scales, tab_words, tab_scales, w1, share, os, vs, offs):
    idx = unstriped(offs)
    keysu = unpack_weight(keys_words, keys_scales, "e4m3")
    tabu = unpack_weight(tab_words, tab_scales, "e4m3")
    queryq = mxq(f64(query), 0, "e4m3")
    keysidxg = keysu[:, idx]
    a = queryq.T @ keysidxg
    query2q = mxq(f64(query2), 0, "e4m3")
    b = query2q.T @ keysidxg
    p = np.exp(a - np.max(a, axis=1, keepdims=True)) * sigmoid(b)
    z = np.sum(p, axis=1, keepdims=True)
    w = p / z
    w1q = mxq(f64(w1), 0, "e4m3")
    tabidxg = tabu[:, idx]
    zh = w1q.T @ tabidxg
    mz = zh.reshape(R, G, I // G).mean(axis=2)
    mzr = np.repeat(mz, I // G, axis=1)
    hv = np.tanh(zh - mzr * f64(share))
    wo1 = w * f64(os)
    wt1 = wo1.T
    hw = hv * f64(vs)
    ht1 = hw.T
    wt1q = mxq(wt1, 0, "e4m3")
    ht1q = mxq(ht1, 0, "e4m3")
    o = wt1q.T @ ht1q
    return o

@@ -1,0 +1,290 @@
+from contextlib import ExitStack
+
+import concourse.mybir as mybir
+from concourse.masks import make_identity
+
+F32 = mybir.dt.float32
+BF16 = mybir.dt.bfloat16
+I32 = mybir.dt.int32
+U32 = mybir.dt.uint32
+U16 = mybir.dt.uint16
+U8 = mybir.dt.uint8
+FP8X4 = mybir.dt.float8_e4m3fn_x4
+ALU = mybir.AluOpType
+ACT = mybir.ActivationFunctionType
+AXIS = mybir.AxisListType
+
+P = 128
+PACK = 4
+D, K, R, T, I, Q = 512, 512, 512, 2048, 512, 128
+PAGE = 16
+PAGES = I // PAGE
+R_TILES = R // P
+HALF = R // 2
+KEY_ROW = 4
+
+FLOPS = 2 * (2 * D * Q * I + K * R * I + I * Q * R)
+
+
+def tile_attend_lrcentred_asked_kernel(
+    tc, query, query2, keys_words, keys_scales, tab_words, tab_scales, w1, share, slot_os, slot_vs, offs, out
+):
+    nc = tc.nc
+    with ExitStack() as ctx:
+        keep = ctx.enter_context(tc.tile_pool(name="keep", bufs=1))
+        ring = ctx.enter_context(tc.tile_pool(name="ring", bufs=2))
+        psum = ctx.enter_context(tc.psum_pool(name="psum", bufs=1))
+        psum2 = ctx.enter_context(tc.psum_pool(name="psum2", bufs=2))
+
+        offsets = keep.tile([P, I // 16], U16, name="offsets")
+        nc.sync.dma_start(offsets[:], offs)
+
+        def load_scales(name, scales, row):
+            pool_bytes = keep.tile([P, T], U8, name=name, tag=name, align_bytes=64)
+            nc.gpsimd.memset(pool_bytes[:].bitcast(I32), 0)
+            for quad in range(4):
+                nc.sync.dma_start(
+                    pool_bytes[32 * quad + row : 32 * quad + row + 4, :].bitcast(I32),
+                    scales[0, 4 * quad : 4 * quad + 4, :].bitcast(I32),
+                )
+            return pool_bytes
+
+        def load_words(name, words):
+            pool_words = keep.tile([P, T], U32, name=name, align_bytes=64)
+            nc.sync.dma_start(pool_words[:].bitcast(I32), words[0].rearrange("p n t -> p (n t)").bitcast(I32))
+            return pool_words
+
+        def load_rows(name, rows):
+            raw = keep.tile([P, PACK, rows.shape[1]], F32, name=name)
+            nc.sync.dma_start(raw[:], rows.rearrange("(p j) c -> p j c", j=PACK))
+            return raw
+
+        def gather(name, window, dtype):
+            listed = keep.tile([P, I], dtype, name=name, align_bytes=64)
+            nc.vector.tensor_copy(listed[:], window[:].indirect(offsets[:]))
+            return listed
+
+        def interleave(copy, grouped, raw):
+            copy(
+                grouped.rearrange("p (c i) j -> p c j i", i=4),
+                raw.rearrange("p j (c i) -> p c j i", i=4),
+            )
+
+        def quantize(name, grouped, width, tag):
+            codes = keep.tile([P, width], U32, name=name + "_codes", tag=tag, align_bytes=64)
+            scales = keep.tile([P, width], U8, name=name + "_scales", align_bytes=64)
+            nc.vector.quantize_mx(codes[:].bitcast(FP8X4), scales[:], grouped.rearrange("p c j -> p (c j)"))
+            return codes, scales
+
+        def load_small(name, shape, rows, source):
+            small = keep.tile(shape, F32, name=name)
+            if rows < P:
+                nc.gpsimd.memset(small[:], 0.0)
+            nc.sync.dma_start(small[0:rows, :], source)
+            return small
+
+        os_cols = keep.tile([P, PACK], F32, name="os_cols")
+        nc.scalar.dma_start(os_cols[:], slot_os.rearrange("o (p t) -> p (o t)", t=PACK))
+        w1_raw = [None, None]
+        w1_raw[0] = load_rows("w1_raw0", w1[:, 0:HALF])
+        tab_scale_pool = load_scales("tab_scale_pool", tab_scales, 0)
+        tab_pool = load_words("tab_pool", tab_words)
+        key_scale_pool = load_scales("key_scale_pool", keys_scales, KEY_ROW)
+        share_rows = load_small("share_rows", [P, P], R_TILES, share.rearrange("(c p) o -> c (p o)", p=P))
+        query2_raw = load_rows("query2_raw", query2)
+        key_pool = load_words("key_pool", keys_words)
+        w1_raw[1] = load_rows("w1_raw1", w1[:, HALF:R])
+        query_raw = load_rows("query_raw", query)
+        vs_cols = load_small("vs_cols", [P, PACK], P, slot_vs.rearrange("o (p t) -> p (o t)", t=PACK))
+
+        identity = keep.tile([P, P], F32, name="identity")
+        make_identity(nc, identity[:])
+
+        share_bank = psum2.tile([P, I], F32, name="share_bank", tag="zh")
+        nc.tensor.transpose(share_bank[:, 0:P], share_rows[:], identity[:])
+        mean_factor = keep.tile([P, R_TILES], F32, name="mean_factor")
+        nc.scalar.mul(mean_factor[:], share_bank[:, 0:R_TILES], -1.0 / PAGE)
+        os_rows = psum.tile([P, PACK, P], F32, name="os_rows")
+        for t in range(PACK):
+            nc.tensor.transpose(os_rows[:, t, :], os_cols[:, t : t + 1].to_broadcast([P, P]), identity[:])
+
+        def quantize_rows(name, copy, raw, tag):
+            width = raw.shape[2]
+            grouped = keep.tile([P, width, PACK], BF16, name=name + "_grouped", tag=name + "_grouped", align_bytes=64)
+            interleave(copy, grouped[:], raw[:])
+            return quantize(name, grouped[:], width, tag)
+
+        tab_scale = gather("tab_scale", tab_scale_pool, U8)
+        w1_first = quantize_rows("w1_first", nc.scalar.copy, w1_raw[0], "tab_scale_pool")
+        tab = gather("tab", tab_pool, U32)
+        key_scale = gather("key_scale", key_scale_pool, U8)
+
+
+        def layer_product(c, w1_codes, w1_scales):
+            cols = slice((c % 2) * P, (c % 2 + 1) * P)
+            zh = psum2.tile([P, I], F32, name="zh", tag="zh")
+            nc.tensor.matmul_mx(
+                zh[:],
+                lhsT=w1_codes[:, cols].bitcast(FP8X4),
+                lhsT_scale=w1_scales[:, cols],
+                rhs=tab[:].bitcast(FP8X4),
+                rhs_scale=tab_scale[:],
+                start=True,
+                stop=True,
+            )
+            return zh
+
+        def page_sums(zh, tag):
+            page_sum = keep.tile([P, PAGES], F32, name="page_sum", tag=tag, align_bytes=64)
+            nc.vector.tensor_reduce(page_sum[:], zh[:].rearrange("r (g m) -> r g m", m=PAGE), AXIS.X, ALU.add)
+            return page_sum
+
+        def tanh_turned(turned, tag):
+            hv = keep.tile([P, P, PACK], F32, name="hv", tag=tag)
+            nc.scalar.activation(hv[:], turned[:].rearrange("p t r -> p r t"), ACT.Tanh)
+            return hv[:]
+
+        def centre_on_vector(c, zh, page_sum):
+            centred = ring.tile([P, I], F32, name="centred")
+            nc.vector.scalar_tensor_tensor(
+                centred[:].rearrange("r (g m) -> r g m", m=PAGE),
+                page_sum[:].unsqueeze(2).to_broadcast([P, PAGES, PAGE]),
+                mean_factor[:, c : c + 1],
+                zh[:].rearrange("r (g m) -> r g m", m=PAGE),
+                ALU.mult,
+                ALU.add,
+            )
+            hv = ring.tile([P, PACK, P], F32, name="hv_rows")
+            nc.scalar.activation(
+                hv[:].rearrange("r t p -> r p t"), centred[:].rearrange("r (p t) -> r p t", t=PACK), ACT.Tanh
+            )
+            turned = psum2.tile([P, PACK, P], F32, name="turned", tag="turned")
+            for t in range(PACK):
+                nc.tensor.transpose(turned[:, t, :], hv[:, t, :], identity[:])
+            return turned[:].rearrange("p t r -> p r t")
+
+        def centre_in_psum(c, zh, page_sum):
+            shift = ring.tile([P, PAGES, PAGE // PACK], F32, name="shift")
+            nc.scalar.activation(
+                shift[:],
+                page_sum[:].unsqueeze(2).to_broadcast([P, PAGES, PAGE // PACK]),
+                ACT.Copy,
+                scale=mean_factor[:, c : c + 1],
+            )
+            dealt = keep.tile([P, PACK, P], F32, name="dealt", tag="dealt")
+            nc.scalar.copy(dealt[:], zh[:].rearrange("r (p t) -> r t p", t=PACK))
+            turned = psum2.tile([P, PACK, P], F32, name="turned", tag="turned")
+            addends = [shift[:].rearrange("r g j -> r (g j)")] * PACK + [dealt[:, t, :] for t in range(PACK)]
+            for n, addend in enumerate(addends):
+                nc.tensor.matmul(
+                    turned[:, n % PACK, :],
+                    addend,
+                    identity[:],
+                    start=(n == 0),
+                    stop=(n == len(addends) - 1),
+                    is_transpose=True,
+                )
+            return turned
+
+        def scale_hv(engine, hv, tag):
+            grouped = keep.tile([P, P, PACK], BF16, name="h_grouped", tag=tag, align_bytes=64)
+            engine.tensor_tensor(grouped[:], hv, vs_cols[:].unsqueeze(1).to_broadcast([P, P, PACK]), ALU.mult)
+            return grouped
+
+        def quantize_h(c, grouped):
+            cols = slice(c * P, (c + 1) * P)
+            nc.vector.quantize_mx(
+                h_codes[:, cols].bitcast(FP8X4), h_scales[:, cols], grouped[:].rearrange("p c j -> p (c j)")
+            )
+
+        def scores(name, codes, scales):
+            bank = psum.tile([P, I], F32, name=name, tag=name)
+            nc.tensor.matmul_mx(
+                bank[:],
+                lhsT=codes[:].bitcast(FP8X4),
+                lhsT_scale=scales[:],
+                rhs=keys[:].bitcast(FP8X4),
+                rhs_scale=key_scale[KEY_ROW:P, :],
+                start=True,
+                stop=True,
+            )
+            return bank
+
+        def by_pairs(bank):
+            return bank[:].rearrange("q (p u e) -> q u p e", u=2, e=2)
+
+        zh0 = layer_product(0, *w1_first)
+        zh1 = layer_product(1, *w1_first)
+        sums0 = page_sums(zh0, "key_scale_pool")
+        query2_mx = quantize_rows("query2", nc.scalar.copy, query2_raw, "query2_codes")
+        turned0 = centre_in_psum(0, zh0, sums0)
+        sums1 = page_sums(zh1, "sums1")
+        keys = gather("keys", key_pool, U32)
+        hv0 = tanh_turned(turned0, "hv0")
+        b = scores("b", *query2_mx)
+        turned1 = centre_in_psum(1, zh1, sums1)
+        gate = keep.tile([P, 2, P, 2], F32, name="gate")
+        nc.scalar.activation(gate[:], by_pairs(b), ACT.Sigmoid)
+
+        w1_second = quantize_rows("w1_second", nc.vector.tensor_copy, w1_raw[1], "w1_second_codes")
+        query_mx = quantize_rows("query", nc.vector.tensor_copy, query_raw, "query_codes")
+        h0 = scale_hv(nc.gpsimd, hv0, "query_grouped")
+        zh2 = layer_product(2, *w1_second)
+        a = scores("a", *query_mx)
+        zh3 = layer_product(3, *w1_second)
+        sums2 = page_sums(zh2, "sums2")
+        neg_max = keep.tile([P, 1], F32, name="neg_max", tag="neg_max")
+        nc.vector.tensor_reduce(neg_max[:], a[:], AXIS.X, ALU.max, negate=True)
+        exp_a = keep.tile([P, 2, P, 2], F32, name="exp_a")
+        nc.scalar.activation(exp_a[:], by_pairs(a), ACT.Exp, bias=neg_max[:])
+        h1 = scale_hv(nc.gpsimd, tanh_turned(turned1, "neg_max"), "h1")
+        sums3 = page_sums(zh3, "sums3")
+        turned2 = centre_on_vector(2, zh2, sums2)
+        turned3 = centre_on_vector(3, zh3, sums3)
+        h_codes = keep.tile([P, R], U32, name="h_codes", tag="sums3", align_bytes=64)
+        h_scales = keep.tile([P, R], U8, name="h_scales", align_bytes=64)
+        quantize_h(0, h0)
+
+        p = keep.tile([P, 2, P, 2], F32, name="p")
+        z = keep.tile([P, 1], F32, name="z")
+        nc.vector.scalar_tensor_tensor(p[:], exp_a[:], 1.0, gate[:], ALU.mult, ALU.mult, accum_out=z[:])
+        inv_z = keep.tile([P, 1], F32, name="inv_z")
+        nc.vector.reciprocal(inv_z[:], z[:])
+        w_pairs = keep.tile([P, 2, P, 2], BF16, name="w_pairs")
+        w_turned = psum.tile([P, 2, P], F32, name="w_turned", tag="b")
+        for u in range(2):
+            nc.vector.scalar_tensor_tensor(
+                w_pairs[:, u, :, :],
+                p[:, u, :, :],
+                inv_z[:],
+                os_rows[:, 2 * u : 2 * u + 2, :].rearrange("q e p -> q p e"),
+                ALU.mult,
+                ALU.mult,
+            )
+            nc.tensor.transpose(
+                w_turned[:, u, :], w_pairs[:, u, :, :].rearrange("q p e -> q (p e)").bitcast(F32), identity[:]
+            )
+        w_grouped = keep.tile([P, Q, PACK], BF16, name="w_grouped", align_bytes=64)
+        nc.scalar.copy(w_grouped[:].bitcast(F32), w_turned[:].rearrange("p u q -> p q u"))
+        h2 = scale_hv(nc.vector, turned2, "h2")
+        h3 = scale_hv(nc.vector, turned3, "h3")
+        quantize_h(1, h1)
+        quantize_h(2, h2)
+        quantize_h(3, h3)
+        w_codes, w_scales = quantize("w", w_grouped[:], Q, "w_codes")
+
+        for half, copy in enumerate((nc.scalar.copy, nc.vector.tensor_copy)):
+            cols = slice(half * HALF, (half + 1) * HALF)
+            bank = psum2.tile([P, HALF], F32, name="out_bank", tag="zh")
+            nc.tensor.matmul_mx(
+                bank[:],
+                lhsT=w_codes[:].bitcast(FP8X4),
+                lhsT_scale=w_scales[:],
+                rhs=h_codes[:, cols].bitcast(FP8X4),
+                rhs_scale=h_scales[:, cols],
+                start=True,
+                stop=True,
+            )
+            result = keep.tile([P, HALF], F32, name="result%d" % half)
+            copy(result[:], bank[:])
+            nc.sync.dma_start(out[:, cols], result[:])

@@ -85,6 +85,9 @@ def tile_attend_lrcentred_asked_kernel(
 
         os_cols = keep.tile([P, PACK], F32, name="os_cols")
         nc.scalar.dma_start(os_cols[:], slot_os.rearrange("o (p t) -> p (o t)", t=PACK))
+        warm = keep.tile([P, 2], F32, name="warm")
+        nc.vector.memset(warm[:, 0:1], 0.0)
+        nc.scalar.activation(warm[:, 1:2], warm[:, 0:1], ACT.Sigmoid)
         w1_raw = [None, None]
         w1_raw[0] = load_rows("w1_raw0", w1[:, 0:HALF])
         tab_scale_pool = load_scales("tab_scale_pool", tab_scales, 0)

from contextlib import ExitStack

import concourse.mybir as mybir
from concourse.masks import make_identity

F32 = mybir.dt.float32
BF16 = mybir.dt.bfloat16
I32 = mybir.dt.int32
U32 = mybir.dt.uint32
U16 = mybir.dt.uint16
U8 = mybir.dt.uint8
FP8X4 = mybir.dt.float8_e4m3fn_x4
ALU = mybir.AluOpType
ACT = mybir.ActivationFunctionType
AXIS = mybir.AxisListType

P = 128
PACK = 4
D, K, R, T, I, Q = 512, 512, 512, 2048, 512, 128
PAGE = 16
PAGES = I // PAGE
R_TILES = R // P
HALF = R // 2
KEY_ROW = 4

FLOPS = 2 * (2 * D * Q * I + K * R * I + I * Q * R)


def tile_attend_lrcentred_asked_kernel(
    tc, query, query2, keys_words, keys_scales, tab_words, tab_scales, w1, share, slot_os, slot_vs, offs, out
):
    nc = tc.nc
    with ExitStack() as ctx:
        keep = ctx.enter_context(tc.tile_pool(name="keep", bufs=1))
        ring = ctx.enter_context(tc.tile_pool(name="ring", bufs=2))
        psum = ctx.enter_context(tc.psum_pool(name="psum", bufs=1))
        psum2 = ctx.enter_context(tc.psum_pool(name="psum2", bufs=2))

        offsets = keep.tile([P, I // 16], U16, name="offsets")
        nc.sync.dma_start(offsets[:], offs)

        def load_scales(name, scales, row):
            pool_bytes = keep.tile([P, T], U8, name=name, tag=name, align_bytes=64)
            nc.gpsimd.memset(pool_bytes[:].bitcast(I32), 0)
            for quad in range(4):
                nc.sync.dma_start(
                    pool_bytes[32 * quad + row : 32 * quad + row + 4, :].bitcast(I32),
                    scales[0, 4 * quad : 4 * quad + 4, :].bitcast(I32),
                )
            return pool_bytes

        def load_words(name, words):
            pool_words = keep.tile([P, T], U32, name=name, align_bytes=64)
            nc.sync.dma_start(pool_words[:].bitcast(I32), words[0].rearrange("p n t -> p (n t)").bitcast(I32))
            return pool_words

        def load_rows(name, rows):
            raw = keep.tile([P, PACK, rows.shape[1]], F32, name=name)
            nc.sync.dma_start(raw[:], rows.rearrange("(p j) c -> p j c", j=PACK))
            return raw

        def gather(name, window, dtype):
            listed = keep.tile([P, I], dtype, name=name, align_bytes=64)
            nc.vector.tensor_copy(listed[:], window[:].indirect(offsets[:]))
            return listed

        def interleave(copy, grouped, raw):
            copy(
                grouped.rearrange("p (c i) j -> p c j i", i=4),
                raw.rearrange("p j (c i) -> p c j i", i=4),
            )

        def quantize(name, grouped, width, tag):
            codes = keep.tile([P, width], U32, name=name + "_codes", tag=tag, align_bytes=64)
            scales = keep.tile([P, width], U8, name=name + "_scales", align_bytes=64)
            nc.vector.quantize_mx(codes[:].bitcast(FP8X4), scales[:], grouped.rearrange("p c j -> p (c j)"))
            return codes, scales

        def load_small(name, shape, rows, source):
            small = keep.tile(shape, F32, name=name)
            if rows < P:
                nc.gpsimd.memset(small[:], 0.0)
            nc.sync.dma_start(small[0:rows, :], source)
            return small

        os_cols = keep.tile([P, PACK], F32, name="os_cols")
        nc.scalar.dma_start(os_cols[:], slot_os.rearrange("o (p t) -> p (o t)", t=PACK))
        warm = keep.tile([P, 2], F32, name="warm")
        nc.vector.memset(warm[:, 0:1], 0.0)
        nc.scalar.activation(warm[:, 1:2], warm[:, 0:1], ACT.Sigmoid)
        w1_raw = [None, None]
        w1_raw[0] = load_rows("w1_raw0", w1[:, 0:HALF])
        tab_scale_pool = load_scales("tab_scale_pool", tab_scales, 0)
        tab_pool = load_words("tab_pool", tab_words)
        key_scale_pool = load_scales("key_scale_pool", keys_scales, KEY_ROW)
        share_rows = load_small("share_rows", [P, P], R_TILES, share.rearrange("(c p) o -> c (p o)", p=P))
        query2_raw = load_rows("query2_raw", query2)
        key_pool = load_words("key_pool", keys_words)
        w1_raw[1] = load_rows("w1_raw1", w1[:, HALF:R])
        query_raw = load_rows("query_raw", query)
        vs_cols = load_small("vs_cols", [P, PACK], P, slot_vs.rearrange("o (p t) -> p (o t)", t=PACK))

        identity = keep.tile([P, P], F32, name="identity")
        make_identity(nc, identity[:])

        share_bank = psum2.tile([P, I], F32, name="share_bank", tag="zh")
        nc.tensor.transpose(share_bank[:, 0:P], share_rows[:], identity[:])
        mean_factor = keep.tile([P, R_TILES], F32, name="mean_factor")
        nc.scalar.mul(mean_factor[:], share_bank[:, 0:R_TILES], -1.0 / PAGE)
        os_rows = psum.tile([P, PACK, P], F32, name="os_rows")
        for t in range(PACK):
            nc.tensor.transpose(os_rows[:, t, :], os_cols[:, t : t + 1].to_broadcast([P, P]), identity[:])

        def quantize_rows(name, copy, raw, tag):
            width = raw.shape[2]
            grouped = keep.tile([P, width, PACK], BF16, name=name + "_grouped", tag=name + "_grouped", align_bytes=64)
            interleave(copy, grouped[:], raw[:])
            return quantize(name, grouped[:], width, tag)

        tab_scale = gather("tab_scale", tab_scale_pool, U8)
        w1_first = quantize_rows("w1_first", nc.scalar.copy, w1_raw[0], "tab_scale_pool")
        tab = gather("tab", tab_pool, U32)
        key_scale = gather("key_scale", key_scale_pool, U8)


        def layer_product(c, w1_codes, w1_scales):
            cols = slice((c % 2) * P, (c % 2 + 1) * P)
            zh = psum2.tile([P, I], F32, name="zh", tag="zh")
            nc.tensor.matmul_mx(
                zh[:],
                lhsT=w1_codes[:, cols].bitcast(FP8X4),
                lhsT_scale=w1_scales[:, cols],
                rhs=tab[:].bitcast(FP8X4),
                rhs_scale=tab_scale[:],
                start=True,
                stop=True,
            )
            return zh

        def page_sums(zh, tag):
            page_sum = keep.tile([P, PAGES], F32, name="page_sum", tag=tag, align_bytes=64)
            nc.vector.tensor_reduce(page_sum[:], zh[:].rearrange("r (g m) -> r g m", m=PAGE), AXIS.X, ALU.add)
            return page_sum

        def tanh_turned(turned, tag):
            hv = keep.tile([P, P, PACK], F32, name="hv", tag=tag)
            nc.scalar.activation(hv[:], turned[:].rearrange("p t r -> p r t"), ACT.Tanh)
            return hv[:]

        def centre_on_vector(c, zh, page_sum):
            centred = ring.tile([P, I], F32, name="centred")
            nc.vector.scalar_tensor_tensor(
                centred[:].rearrange("r (g m) -> r g m", m=PAGE),
                page_sum[:].unsqueeze(2).to_broadcast([P, PAGES, PAGE]),
                mean_factor[:, c : c + 1],
                zh[:].rearrange("r (g m) -> r g m", m=PAGE),
                ALU.mult,
                ALU.add,
            )
            hv = ring.tile([P, PACK, P], F32, name="hv_rows")
            nc.scalar.activation(
                hv[:].rearrange("r t p -> r p t"), centred[:].rearrange("r (p t) -> r p t", t=PACK), ACT.Tanh
            )
            turned = psum2.tile([P, PACK, P], F32, name="turned", tag="turned")
            for t in range(PACK):
                nc.tensor.transpose(turned[:, t, :], hv[:, t, :], identity[:])
            return turned[:].rearrange("p t r -> p r t")

        def centre_in_psum(c, zh, page_sum):
            shift = ring.tile([P, PAGES, PAGE // PACK], F32, name="shift")
            nc.scalar.activation(
                shift[:],
                page_sum[:].unsqueeze(2).to_broadcast([P, PAGES, PAGE // PACK]),
                ACT.Copy,
                scale=mean_factor[:, c : c + 1],
            )
            dealt = keep.tile([P, PACK, P], F32, name="dealt", tag="dealt")
            nc.scalar.copy(dealt[:], zh[:].rearrange("r (p t) -> r t p", t=PACK))
            turned = psum2.tile([P, PACK, P], F32, name="turned", tag="turned")
            addends = [shift[:].rearrange("r g j -> r (g j)")] * PACK + [dealt[:, t, :] for t in range(PACK)]
            for n, addend in enumerate(addends):
                nc.tensor.matmul(
                    turned[:, n % PACK, :],
                    addend,
                    identity[:],
                    start=(n == 0),
                    stop=(n == len(addends) - 1),
                    is_transpose=True,
                )
            return turned

        def scale_hv(engine, hv, tag):
            grouped = keep.tile([P, P, PACK], BF16, name="h_grouped", tag=tag, align_bytes=64)
            engine.tensor_tensor(grouped[:], hv, vs_cols[:].unsqueeze(1).to_broadcast([P, P, PACK]), ALU.mult)
            return grouped

        def quantize_h(c, grouped):
            cols = slice(c * P, (c + 1) * P)
            nc.vector.quantize_mx(
                h_codes[:, cols].bitcast(FP8X4), h_scales[:, cols], grouped[:].rearrange("p c j -> p (c j)")
            )

        def scores(name, codes, scales):
            bank = psum.tile([P, I], F32, name=name, tag=name)
            nc.tensor.matmul_mx(
                bank[:],
                lhsT=codes[:].bitcast(FP8X4),
                lhsT_scale=scales[:],
                rhs=keys[:].bitcast(FP8X4),
                rhs_scale=key_scale[KEY_ROW:P, :],
                start=True,
                stop=True,
            )
            return bank

        def by_pairs(bank):
            return bank[:].rearrange("q (p u e) -> q u p e", u=2, e=2)

        zh0 = layer_product(0, *w1_first)
        zh1 = layer_product(1, *w1_first)
        sums0 = page_sums(zh0, "key_scale_pool")
        query2_mx = quantize_rows("query2", nc.scalar.copy, query2_raw, "query2_codes")
        turned0 = centre_in_psum(0, zh0, sums0)
        sums1 = page_sums(zh1, "sums1")
        keys = gather("keys", key_pool, U32)
        hv0 = tanh_turned(turned0, "hv0")
        b = scores("b", *query2_mx)
        turned1 = centre_in_psum(1, zh1, sums1)
        gate = keep.tile([P, 2, P, 2], F32, name="gate")
        nc.scalar.activation(gate[:], by_pairs(b), ACT.Sigmoid)

        w1_second = quantize_rows("w1_second", nc.vector.tensor_copy, w1_raw[1], "w1_second_codes")
        query_mx = quantize_rows("query", nc.vector.tensor_copy, query_raw, "query_codes")
        h0 = scale_hv(nc.gpsimd, hv0, "query_grouped")
        zh2 = layer_product(2, *w1_second)
        a = scores("a", *query_mx)
        zh3 = layer_product(3, *w1_second)
        sums2 = page_sums(zh2, "sums2")
        neg_max = keep.tile([P, 1], F32, name="neg_max", tag="neg_max")
        nc.vector.tensor_reduce(neg_max[:], a[:], AXIS.X, ALU.max, negate=True)
        exp_a = keep.tile([P, 2, P, 2], F32, name="exp_a")
        nc.scalar.activation(exp_a[:], by_pairs(a), ACT.Exp, bias=neg_max[:])
        h1 = scale_hv(nc.gpsimd, tanh_turned(turned1, "neg_max"), "h1")
        sums3 = page_sums(zh3, "sums3")
        turned2 = centre_on_vector(2, zh2, sums2)
        turned3 = centre_on_vector(3, zh3, sums3)
        h_codes = keep.tile([P, R], U32, name="h_codes", tag="sums3", align_bytes=64)
        h_scales = keep.tile([P, R], U8, name="h_scales", align_bytes=64)
        quantize_h(0, h0)

        p = keep.tile([P, 2, P, 2], F32, name="p")
        z = keep.tile([P, 1], F32, name="z")
        nc.vector.scalar_tensor_tensor(p[:], exp_a[:], 1.0, gate[:], ALU.mult, ALU.mult, accum_out=z[:])
        inv_z = keep.tile([P, 1], F32, name="inv_z")
        nc.vector.reciprocal(inv_z[:], z[:])
        w_pairs = keep.tile([P, 2, P, 2], BF16, name="w_pairs")
        w_turned = psum.tile([P, 2, P], F32, name="w_turned", tag="b")
        for u in range(2):
            nc.vector.scalar_tensor_tensor(
                w_pairs[:, u, :, :],
                p[:, u, :, :],
                inv_z[:],
                os_rows[:, 2 * u : 2 * u + 2, :].rearrange("q e p -> q p e"),
                ALU.mult,
                ALU.mult,
            )
            nc.tensor.transpose(
                w_turned[:, u, :], w_pairs[:, u, :, :].rearrange("q p e -> q (p e)").bitcast(F32), identity[:]
            )
        w_grouped = keep.tile([P, Q, PACK], BF16, name="w_grouped", align_bytes=64)
        nc.scalar.copy(w_grouped[:].bitcast(F32), w_turned[:].rearrange("p u q -> p q u"))
        h2 = scale_hv(nc.vector, turned2, "h2")
        h3 = scale_hv(nc.vector, turned3, "h3")
        quantize_h(1, h1)
        quantize_h(2, h2)
        quantize_h(3, h3)
        w_codes, w_scales = quantize("w", w_grouped[:], Q, "w_codes")

        for half, copy in enumerate((nc.scalar.copy, nc.vector.tensor_copy)):
            cols = slice(half * HALF, (half + 1) * HALF)
            bank = psum2.tile([P, HALF], F32, name="out_bank", tag="zh")
            nc.tensor.matmul_mx(
                bank[:],
                lhsT=w_codes[:].bitcast(FP8X4),
                lhsT_scale=w_scales[:],
                rhs=h_codes[:, cols].bitcast(FP8X4),
                rhs_scale=h_scales[:, cols],
                start=True,
                stop=True,
            )
            result = keep.tile([P, HALF], F32, name="result%d" % half)
            copy(result[:], bank[:])
            nc.sync.dma_start(out[:, cols], result[:])
